import numpy as np
import ml_dtypes


def mxq(x, axis, fmt="e4m3"):
    dtype, down = {"e4m3": (ml_dtypes.float8_e4m3fn, 7), "e5m2": (ml_dtypes.float8_e5m2, 14)}[fmt]
    v = np.moveaxis(np.asarray(x, np.float32).astype(ml_dtypes.bfloat16).astype(np.float64), axis, -1)
    blocks = v.reshape(v.shape[:-1] + (-1, 32))
    amax = np.abs(blocks).max(-1, keepdims=True)
    byte = np.maximum(np.where(amax > 0, np.frexp(amax)[1] - 1 + 127, 0) - down, 1)
    scale = np.exp2(byte - 127.0)
    codes = (blocks / scale).astype(np.float32).astype(dtype).astype(np.float64)
    return np.moveaxis((codes * scale).reshape(v.shape), -1, axis)


WIDE = False


def mx_kscale(k):
    if not WIDE:
        return np.ones(k)
    levels = np.array([10, -10, 5, -5, 0])
    if k % 512:
        return np.exp2(np.random.permutation(np.resize(levels, k // 32))).repeat(32)
    a = np.empty((k // 512, 16))
    for p in range(k // 512):
        a[p, :8] = np.random.permutation(np.resize(levels, 8))
        for g in range(8):
            far = levels[np.abs(levels - a[p, g]) >= 10]
            a[p, g + 8] = far[np.random.randint(len(far))]
    return np.exp2(a.ravel()).repeat(32)


def f64(x):
    return np.asarray(x).astype(np.float64)


def striped(idx):
    return np.tile(idx.reshape(-1, 16).T, (8, 1)).astype(np.uint16)


def unstriped(offs):
    return offs[:16].T.reshape(-1).astype(np.int64)


E2M1 = np.array([0.0, 0.5, 1.0, 1.5, 2.0, 3.0, 4.0, 6.0, -0.0, -0.5, -1.0, -1.5, -2.0, -3.0, -4.0, -6.0])


def pack_weight(w, fmt):
    k, n = w.shape
    w = f64(np.asarray(w, np.float32).astype(ml_dtypes.bfloat16)).reshape(k // 32, 32, n)
    amax = np.abs(w).max(1)
    if fmt == "e4m3":
        byte = np.frexp(amax)[1] - 1 + 127 - 7
    else:
        mant, ex = np.frexp(amax / 6.0)
        byte = np.where(mant > 0.5, ex, ex - 1) + 127
    byte = np.clip(np.where(amax > 0, byte, 1), 1, 254)
    scaled = (w * np.exp2(127.0 - byte)[:, None, :]).reshape(k, n).astype(np.float32)
    by_word = np.ascontiguousarray(scaled.reshape(k // 512, 128, 4, n).transpose(0, 1, 3, 2))
    if fmt == "e4m3":
        words = by_word.astype(ml_dtypes.float8_e4m3fn).view(np.uint8)
    else:
        c = by_word.astype(ml_dtypes.float4_e2m1fn).view(np.uint8) & 0xF
        words = (c[..., 0::2] | (c[..., 1::2] << 4)).reshape(k // 512, 128, 2 * n)
    return np.ascontiguousarray(words), np.ascontiguousarray(byte.astype(np.uint8).reshape(k // 512, 16, n))


def unpack_weight(words, scales, fmt):
    g, _, n = scales.shape
    words = np.ascontiguousarray(words).reshape(g, 128, n, -1)
    if fmt == "e4m3":
        vals = words.view(ml_dtypes.float8_e4m3fn).astype(np.float64)
    else:
        nib = np.empty((g, 128, n, 4), np.uint8)
        nib[..., 0::2] = words & 0xF
        nib[..., 1::2] = words >> 4
        vals = E2M1[nib]
    vals = vals * np.repeat(np.exp2(scales.astype(np.float64) - 127.0), 8, axis=1)[..., None]
    return vals.transpose(0, 1, 3, 2).reshape(g * 512, n)


def sigmoid(v):
    return 1.0 / (1.0 + np.exp(-np.maximum(v, -700.0)))


K, T, E1, C1, E2, C2, H = 512, 768, 6, 128, 3, 256, 512
N = 256


def by_expert(wq, xq, E, C):
    return np.concatenate([wq[e].T @ xq[:, e * C:(e + 1) * C] for e in range(E)], axis=1)


def setup_inputs():
    n = np.random.standard_normal
    s = mx_kscale(K)
    u = mx_kscale(H)
    slots1, slots2 = np.random.permutation(T), np.random.permutation(T)
    x = pack_weight(n((K, T)) * s[:, None], "e4m3")
    wa = [pack_weight(m, "e2m1") for m in n((E1, K, H)) / np.sqrt(K) / s[None, :, None]]
    wb = [pack_weight(m, "e2m1") for m in n((E2, K, H)) / np.sqrt(K) / s[None, :, None] * u]
    w2 = pack_weight(n((H, N)) / np.sqrt(H) / u[:, None], "e2m1")
    return {
        "x_words": x[0],
        "x_scales": x[1],
        "wa_words": np.stack([m[0] for m in wa]),
        "wa_scales": np.stack([m[1] for m in wa]),
        "wb_words": np.stack([m[0] for m in wb]),
        "wb_scales": np.stack([m[1] for m in wb]),
        "w2_words": w2[0],
        "w2_scales": w2[1],
        "offs": striped(slots1),
        "offs2": striped(slots2),
    }


def reference(x_words, x_scales, wa_words, wa_scales, wb_words, wb_scales, w2_words, w2_scales, offs, offs2):
    wa = np.stack([unpack_weight(wa_words[e], wa_scales[e], "e2m1") for e in range(E1)])
    wb = np.stack([unpack_weight(wb_words[e], wb_scales[e], "e2m1") for e in range(E2)])
    w2 = unpack_weight(w2_words, w2_scales, "e2m1")
    idx, idx2 = unstriped(offs), unstriped(offs2)
    x = unpack_weight(x_words, x_scales, "e4m3")
    a, c = np.zeros((H, T)), np.zeros((H, T))
    a[:, idx] = by_expert(wa, x[:, idx], E1, C1)
    c[:, idx2] = by_expert(wb, x[:, idx2], E2, C2)
    return w2.T @ mxq(sigmoid(a) * c, 0, "e4m3")

@@ -1,0 +1,146 @@
+from contextlib import ExitStack
+
+import concourse.mybir as mybir
+from concourse.masks import make_identity
+
+K, T, E1, C1, E2, C2, H, N = 512, 768, 6, 128, 3, 256, 512, 256
+FLOPS = 2 * T * (2 * K * H + H * N)
+
+F32 = mybir.dt.float32
+BF16 = mybir.dt.bfloat16
+I32 = mybir.dt.int32
+U32 = mybir.dt.uint32
+U16 = mybir.dt.uint16
+U8 = mybir.dt.uint8
+FP8X4 = mybir.dt.float8_e4m3fn_x4
+FP4X4 = mybir.dt.float4_e2m1fn_x4
+SIGMOID = mybir.ActivationFunctionType.Sigmoid
+MULT = mybir.AluOpType.mult
+
+P = 128
+PACK = 4
+LIST_ROWS = 16
+SLOT_TILES = T // P
+
+
+def load_scales(nc, plane, rows):
+    for q in range(4):
+        nc.sync.dma_start(out=plane[32 * q : 32 * q + 4].bitcast(I32), in_=rows[4 * q : 4 * q + 4].bitcast(I32))
+
+
+def offsets(lst, lo, hi):
+    return lst[:, lo // LIST_ROWS : hi // LIST_ROWS]
+
+
+def tile_moe_pool_sigmoid_kernel(
+    tc, x_words, x_scales, wa_words, wa_scales, wb_words, wb_scales, w2_words, w2_scales, offs, offs2, out
+):
+    nc = tc.nc
+    with ExitStack() as ctx:
+        keep = ctx.enter_context(tc.tile_pool(name="keep", bufs=1))
+        stage = ctx.enter_context(tc.tile_pool(name="stage", bufs=3))
+        psum = ctx.enter_context(tc.psum_pool(name="psum", bufs=1))
+
+        list_a = keep.tile([P, T // LIST_ROWS], U16, name="list_a")
+        list_b = keep.tile([P, T // LIST_ROWS], U16, name="list_b")
+        xw = keep.tile([P, T], I32, name="xw", align_bytes=64)
+        xs = keep.tile([P, T], U8, name="xs", align_bytes=64)
+        wa = keep.tile([P, E1, 2 * H], U8, name="wa", align_bytes=64)
+        wb = keep.tile([P, E2, 2 * H], U8, name="wb", align_bytes=64)
+        w2 = keep.tile([P, 2 * N], U8, name="w2", align_bytes=64)
+        was = keep.tile([P, E1, H], U8, name="was", align_bytes=64)
+        wbs = keep.tile([P, E2, H], U8, name="wbs", align_bytes=64)
+        w2s = keep.tile([P, N], U8, name="w2s", align_bytes=64)
+        ident = keep.tile([P, P], F32, name="ident")
+
+        nc.vector.memset(xs[:].bitcast(I32), 0)
+        nc.vector.memset(was[:].bitcast(I32), 0)
+        nc.vector.memset(wbs[:].bitcast(I32), 0)
+        nc.vector.memset(w2s[:].bitcast(I32), 0)
+        make_identity(nc, ident[:])
+
+        nc.sync.dma_start(list_a[:], offs)
+        nc.sync.dma_start(out=xw[:], in_=x_words.rearrange("s p t d -> p (s t d)").bitcast(I32))
+        load_scales(nc, xs, x_scales[0])
+        nc.sync.dma_start(list_b[:], offs2)
+        wa_rows = wa_words.rearrange("e s p b -> p (e s) b")
+        nc.sync.dma_start(out=wa[:, 0:2, :].bitcast(I32), in_=wa_rows[:, 0:2, :].bitcast(I32))
+        load_scales(nc, was, wa_scales.rearrange("e s r n -> r (e s) n"))
+        nc.sync.dma_start(out=wa[:, 2:E1, :].bitcast(I32), in_=wa_rows[:, 2:E1, :].bitcast(I32))
+        nc.sync.dma_start(out=wb[:].bitcast(I32), in_=wb_words.rearrange("e s p b -> p (e s) b").bitcast(I32))
+        load_scales(nc, wbs, wb_scales.rearrange("e s r n -> r (e s) n"))
+        nc.sync.dma_start(out=w2[:].bitcast(I32), in_=w2_words[0].bitcast(I32))
+        load_scales(nc, w2s, w2_scales[0])
+
+        pools = []
+        for name, lst, cuts in (("a", list_a, (0, 256, T)), ("b", list_b, (0, 384, T))):
+            gw = keep.tile([P, T], U32, name="gw_" + name, align_bytes=64)
+            gs = keep.tile([P, T], U8, name="gs_" + name, align_bytes=64)
+            for lo, hi in zip(cuts, cuts[1:]):
+                nc.vector.tensor_copy(gw[:, lo:hi], xw[:].bitcast(U32).indirect(offsets(lst, lo, hi)))
+                nc.vector.tensor_copy(gs[:, lo:hi], xs[:].indirect(offsets(lst, lo, hi)))
+            pools.append((gw, gs))
+
+        slot_vals = []
+        for pool, (gw, gs) in enumerate(pools):
+            words, scales, per = ((wa, was, C1), (wb, wbs, C2))[pool]
+            vals = keep.tile([P, PACK, T], F32, name="vals%d" % pool)
+            for s in range(SLOT_TILES):
+                cols = slice(s * P, (s + 1) * P)
+                e = s * P // per
+                acc = psum.tile([P, H], F32, name="acc", tag="acc", bufs=3)
+                nc.tensor.matmul_mx(
+                    out=acc[:], lhsT=gw[:, cols].bitcast(FP8X4), lhsT_scale=gs[:, cols],
+                    rhs=words[:, e, :].bitcast(FP4X4), rhs_scale=scales[:, e, :], start=True, stop=True,
+                )
+                rows = stage.tile([P, PACK, P], F32, name="rows")
+                src = acc[:].rearrange("p (m t) -> p t m", t=PACK)
+                if pool == 0:
+                    nc.scalar.activation(rows[:], src, SIGMOID)
+                else:
+                    nc.scalar.copy(rows[:], src)
+                turned = psum.tile([P, PACK, P], F32, name="turned", tag="turned", bufs=3)
+                for t in range(PACK):
+                    nc.tensor.transpose(turned[:, t, :], rows[:, t, :], ident[:])
+                nc.scalar.copy(vals[:, :, cols], turned[:])
+            slot_vals.append(vals)
+
+        gate = [keep.tile([P, T], F32, name="gate%d" % t) for t in range(PACK)]
+        lin = [keep.tile([P, T], F32, name="lin%d" % t) for t in range(PACK)]
+        for lo, hi in ((0, 256), (256, T)):
+            for t in range(PACK):
+                nc.vector.tensor_copy(gate[t][:].indirect(offsets(list_a, lo, hi)), slot_vals[0][:, t, lo:hi])
+        hb = keep.tile([P, PACK, T], BF16, name="hb", align_bytes=64)
+        for t in range(PACK):
+            for lo, hi in ((0, 384), (384, T)):
+                nc.vector.tensor_copy(lin[t][:].indirect(offsets(list_b, lo, hi)), slot_vals[1][:, t, lo:hi])
+            if t < PACK - 1:
+                nc.gpsimd.tensor_tensor(hb[:, t, :], gate[t][:], lin[t][:], MULT)
+
+        chunk = 256
+        chunks = [slice(c, c + chunk) for c in range(0, T, chunk)]
+        last = PACK - 1
+        for cols in (chunks[2], chunks[0], chunks[1]):
+            nc.vector.tensor_tensor(hb[:, last, cols], gate[last][:, cols], lin[last][:, cols], MULT)
+        grouped = [keep.tile([P, chunk, PACK], BF16, name="grouped%d" % c, align_bytes=64) for c in range(3)]
+        for c in (2, 0, 1):
+            dst = grouped[c][:].rearrange("p (c i) t -> p c t i", i=4)
+            src = hb[:, :, chunks[c]].rearrange("p t (c i) -> p c t i", i=4)
+            if c == 2:
+                nc.scalar.copy(dst, src)
+            else:
+                nc.vector.tensor_copy(dst, src)
+        out_rows = out.rearrange("(u p) t -> p u t", p=P)
+        for c, cols in enumerate(chunks):
+            hq = keep.tile([P, chunk], U32, name="hq%d" % c, align_bytes=64)
+            hs = keep.tile([P, chunk], U8, name="hs%d" % c, align_bytes=64)
+            nc.vector.quantize_mx(out=hq[:].bitcast(FP8X4), scales=hs[:], in_=grouped[c][:].rearrange("p k t -> p (k t)"))
+            res = psum.tile([P, 2, chunk], F32, name="res", tag="res", bufs=2)
+            for u in range(2):
+                nc.tensor.matmul_mx(
+                    out=res[:, u, :], lhsT=w2[:, 2 * P * u : 2 * P * (u + 1)].bitcast(FP4X4), lhsT_scale=w2s[:, P * u : P * (u + 1)],
+                    rhs=hq[:].bitcast(FP8X4), rhs_scale=hs[:], start=True, stop=True,
+                )
+            done = stage.tile([P, 2, chunk], F32, name="done")
+            nc.scalar.copy(done[:], res[:])
+            nc.sync.dma_start(out=out_rows[:, :, cols], in_=done[:])

@@ -21,11 +21,12 @@ P = 128
 PACK = 4
 LIST_ROWS = 16
 SLOT_TILES = T // P
+WINDOW = 1024
 
 
-def load_scales(nc, plane, rows):
+def load_scales(queue, plane, rows):
     for q in range(4):
-        nc.sync.dma_start(out=plane[32 * q : 32 * q + 4].bitcast(I32), in_=rows[4 * q : 4 * q + 4].bitcast(I32))
+        queue.dma_start(out=plane[32 * q : 32 * q + 4].bitcast(I32), in_=rows[4 * q : 4 * q + 4].bitcast(I32))
 
 
 def offsets(lst, lo, hi):
@@ -53,32 +54,33 @@ def tile_moe_pool_sigmoid_kernel(
         w2s = keep.tile([P, N], U8, name="w2s", align_bytes=64)
         ident = keep.tile([P, P], F32, name="ident")
 
-        nc.vector.memset(xs[:].bitcast(I32), 0)
+        nc.gpsimd.memset(xs[:].bitcast(I32), 0)
         nc.vector.memset(was[:].bitcast(I32), 0)
-        nc.vector.memset(wbs[:].bitcast(I32), 0)
-        nc.vector.memset(w2s[:].bitcast(I32), 0)
         make_identity(nc, ident[:])
+        nc.gpsimd.memset(wbs[:].bitcast(I32), 0)
+        nc.gpsimd.memset(w2s[:].bitcast(I32), 0)
 
         nc.sync.dma_start(list_a[:], offs)
         nc.sync.dma_start(out=xw[:], in_=x_words.rearrange("s p t d -> p (s t d)").bitcast(I32))
-        load_scales(nc, xs, x_scales[0])
-        nc.sync.dma_start(list_b[:], offs2)
+        load_scales(nc.scalar, xs, x_scales[0])
+        load_scales(nc.sync, was, wa_scales.rearrange("e s r n -> r (e s) n"))
         wa_rows = wa_words.rearrange("e s p b -> p (e s) b")
         nc.sync.dma_start(out=wa[:, 0:2, :].bitcast(I32), in_=wa_rows[:, 0:2, :].bitcast(I32))
-        load_scales(nc, was, wa_scales.rearrange("e s r n -> r (e s) n"))
+        nc.sync.dma_start(list_b[:], offs2)
         nc.sync.dma_start(out=wa[:, 2:E1, :].bitcast(I32), in_=wa_rows[:, 2:E1, :].bitcast(I32))
         nc.sync.dma_start(out=wb[:].bitcast(I32), in_=wb_words.rearrange("e s p b -> p (e s) b").bitcast(I32))
-        load_scales(nc, wbs, wb_scales.rearrange("e s r n -> r (e s) n"))
+        load_scales(nc.sync, wbs, wb_scales.rearrange("e s r n -> r (e s) n"))
         nc.sync.dma_start(out=w2[:].bitcast(I32), in_=w2_words[0].bitcast(I32))
-        load_scales(nc, w2s, w2_scales[0])
+        load_scales(nc.sync, w2s, w2_scales[0])
 
         pools = []
-        for name, lst, cuts in (("a", list_a, (0, 256, T)), ("b", list_b, (0, 384, T))):
+        for name, lst, cut in (("a", list_a, 256), ("b", list_b, 384)):
             gw = keep.tile([P, T], U32, name="gw_" + name, align_bytes=64)
             gs = keep.tile([P, T], U8, name="gs_" + name, align_bytes=64)
-            for lo, hi in zip(cuts, cuts[1:]):
-                nc.vector.tensor_copy(gw[:, lo:hi], xw[:].bitcast(U32).indirect(offsets(lst, lo, hi)))
+            for lo, hi in ((0, 384), (384, T)):
                 nc.vector.tensor_copy(gs[:, lo:hi], xs[:].indirect(offsets(lst, lo, hi)))
+            for lo, hi in ((0, cut), (cut, T)):
+                nc.vector.tensor_copy(gw[:, lo:hi], xw[:].bitcast(U32).indirect(offsets(lst, lo, hi)))
             pools.append((gw, gs))
 
         slot_vals = []
@@ -106,41 +108,68 @@ def tile_moe_pool_sigmoid_kernel(
             slot_vals.append(vals)
 
         gate = [keep.tile([P, T], F32, name="gate%d" % t) for t in range(PACK)]
-        lin = [keep.tile([P, T], F32, name="lin%d" % t) for t in range(PACK)]
+        lin = [keep.tile([P, WINDOW], F32, name="lin%d" % t) for t in range(PACK)]
         for lo, hi in ((0, 256), (256, T)):
             for t in range(PACK):
                 nc.vector.tensor_copy(gate[t][:].indirect(offsets(list_a, lo, hi)), slot_vals[0][:, t, lo:hi])
         hb = keep.tile([P, PACK, T], BF16, name="hb", align_bytes=64)
-        for t in range(PACK):
-            for lo, hi in ((0, 384), (384, T)):
-                nc.vector.tensor_copy(lin[t][:].indirect(offsets(list_b, lo, hi)), slot_vals[1][:, t, lo:hi])
-            if t < PACK - 1:
-                nc.gpsimd.tensor_tensor(hb[:, t, :], gate[t][:], lin[t][:], MULT)
-
-        chunk = 256
-        chunks = [slice(c, c + chunk) for c in range(0, T, chunk)]
+        grouped = keep.tile([P, T, PACK], BF16, name="grouped", align_bytes=64)
         last = PACK - 1
-        for cols in (chunks[2], chunks[0], chunks[1]):
+        for t in range(PACK):
+            nc.vector.tensor_copy(lin[t][:].indirect(list_b[:]), slot_vals[1][:, t, :])
+            if t < last:
+                nc.gpsimd.tensor_tensor(hb[:, t, :], gate[t][:], lin[t][:, 0:T], MULT)
+            if t == 1:
+                nc.scalar.copy(grouped[:, :, 0:2], hb[:, 0:2, :].rearrange("p t k -> p k t"))
+
+        chunks = [slice(0, 256), slice(256, 512), slice(512, 640), slice(640, T)]
+        out_rows = out.rearrange("(u p) t -> p u t", p=P)
+
+        def product(cols):
             nc.vector.tensor_tensor(hb[:, last, cols], gate[last][:, cols], lin[last][:, cols], MULT)
-        grouped = [keep.tile([P, chunk, PACK], BF16, name="grouped%d" % c, align_bytes=64) for c in range(3)]
-        for c in (2, 0, 1):
-            dst = grouped[c][:].rearrange("p (c i) t -> p c t i", i=4)
-            src = hb[:, :, chunks[c]].rearrange("p t (c i) -> p c t i", i=4)
-            if c == 2:
+
+        def pair(c):
+            dst, src = grouped[:, chunks[c], 2:4], hb[:, 2:4, chunks[c]].rearrange("p t k -> p k t")
+            if c % 2:
                 nc.scalar.copy(dst, src)
             else:
                 nc.vector.tensor_copy(dst, src)
-        out_rows = out.rearrange("(u p) t -> p u t", p=P)
-        for c, cols in enumerate(chunks):
-            hq = keep.tile([P, chunk], U32, name="hq%d" % c, align_bytes=64)
-            hs = keep.tile([P, chunk], U8, name="hs%d" % c, align_bytes=64)
-            nc.vector.quantize_mx(out=hq[:].bitcast(FP8X4), scales=hs[:], in_=grouped[c][:].rearrange("p k t -> p (k t)"))
-            res = psum.tile([P, 2, chunk], F32, name="res", tag="res", bufs=2)
+
+        def finish(c):
+            cols = chunks[c]
+            width = cols.stop - cols.start
+            hq = keep.tile([P, width], U32, name="hq%d" % c, align_bytes=64)
+            hs = keep.tile([P, width], U8, name="hs%d" % c, align_bytes=64)
+            nc.vector.quantize_mx(out=hq[:].bitcast(FP8X4), scales=hs[:], in_=grouped[:, cols, :].rearrange("p k t -> p (k t)"))
+            res = psum.tile([P, 2, width], F32, name="res%d" % c)  if c < 2 else psum.tile([P, 2, width], F32, name="res%d" % c, tag="acc", bufs=3)
             for u in range(2):
                 nc.tensor.matmul_mx(
                     out=res[:, u, :], lhsT=w2[:, 2 * P * u : 2 * P * (u + 1)].bitcast(FP4X4), lhsT_scale=w2s[:, P * u : P * (u + 1)],
                     rhs=hq[:].bitcast(FP8X4), rhs_scale=hs[:], start=True, stop=True,
                 )
-            done = stage.tile([P, 2, chunk], F32, name="done")
-            nc.scalar.copy(done[:], res[:])
+            return res
+
+        def store(c, res):
+            cols = chunks[c]
+            done = keep.tile([P, 2, cols.stop - cols.start], F32, name="done%d" % c)
+            if c < 2:
+                nc.scalar.copy(done[:], res[:])
+            else:
+                nc.vector.tensor_copy(done[:], res[:])
             nc.sync.dma_start(out=out_rows[:, :, cols], in_=done[:])
+
+        product(chunks[0])
+        product(chunks[1])
+        pair(0)
+        pair(1)
+        product(slice(512, T))
+        res0 = finish(0)
+        pair(2)
+        pair(3)
+        store(0, res0)
+        res1 = finish(1)
+        store(1, res1)
+        res2 = finish(2)
+        res3 = finish(3)
+        store(2, res2)
+        store(3, res3)

@@ -22,10 +22,11 @@ PACK = 4
 LIST_ROWS = 16
 SLOT_TILES = T // P
 WINDOW = 1024
+WARM_TRANSPOSES = 14
 
 
-def load_scales(queue, plane, rows):
-    for q in range(4):
+def load_scales(queues, plane, rows):
+    for q, queue in enumerate(queues):
         queue.dma_start(out=plane[32 * q : 32 * q + 4].bitcast(I32), in_=rows[4 * q : 4 * q + 4].bitcast(I32))
 
 
@@ -44,8 +45,8 @@ def tile_moe_pool_sigmoid_kernel(
 
         list_a = keep.tile([P, T // LIST_ROWS], U16, name="list_a")
         list_b = keep.tile([P, T // LIST_ROWS], U16, name="list_b")
-        xw = keep.tile([P, T], I32, name="xw", align_bytes=64)
-        xs = keep.tile([P, T], U8, name="xs", align_bytes=64)
+        xw = keep.tile([P, WINDOW], I32, name="xw", align_bytes=64)
+        xs = keep.tile([P, WINDOW], U8, name="xs", align_bytes=64)
         wa = keep.tile([P, E1, 2 * H], U8, name="wa", align_bytes=64)
         wb = keep.tile([P, E2, 2 * H], U8, name="wb", align_bytes=64)
         w2 = keep.tile([P, 2 * N], U8, name="w2", align_bytes=64)
@@ -54,32 +55,31 @@ def tile_moe_pool_sigmoid_kernel(
         w2s = keep.tile([P, N], U8, name="w2s", align_bytes=64)
         ident = keep.tile([P, P], F32, name="ident")
 
+        wa_rows = wa_words.rearrange("e s p b -> p (e s) b")
         nc.gpsimd.memset(xs[:].bitcast(I32), 0)
         nc.vector.memset(was[:].bitcast(I32), 0)
         make_identity(nc, ident[:])
+        nc.gpsimd.dma_start(out=wa[:, 2:E1, :].bitcast(I32), in_=wa_rows[:, 2:E1, :].bitcast(I32))
         nc.gpsimd.memset(wbs[:].bitcast(I32), 0)
+        nc.gpsimd.dma_start(out=wb[:].bitcast(I32), in_=wb_words.rearrange("e s p b -> p (e s) b").bitcast(I32))
         nc.gpsimd.memset(w2s[:].bitcast(I32), 0)
+        nc.gpsimd.dma_start(out=w2[:].bitcast(I32), in_=w2_words[0].bitcast(I32))
 
         nc.sync.dma_start(list_a[:], offs)
-        nc.sync.dma_start(out=xw[:], in_=x_words.rearrange("s p t d -> p (s t d)").bitcast(I32))
-        load_scales(nc.scalar, xs, x_scales[0])
-        load_scales(nc.sync, was, wa_scales.rearrange("e s r n -> r (e s) n"))
-        wa_rows = wa_words.rearrange("e s p b -> p (e s) b")
+        load_scales((nc.scalar, nc.scalar, nc.sync, nc.sync), xs[:, 0:T], x_scales[0])
+        nc.sync.dma_start(out=xw[:, 0:T], in_=x_words.rearrange("s p t d -> p (s t d)").bitcast(I32))
         nc.sync.dma_start(out=wa[:, 0:2, :].bitcast(I32), in_=wa_rows[:, 0:2, :].bitcast(I32))
+        load_scales((nc.sync,) * 4, was, wa_scales.rearrange("e s r n -> r (e s) n"))
         nc.sync.dma_start(list_b[:], offs2)
-        nc.sync.dma_start(out=wa[:, 2:E1, :].bitcast(I32), in_=wa_rows[:, 2:E1, :].bitcast(I32))
-        nc.sync.dma_start(out=wb[:].bitcast(I32), in_=wb_words.rearrange("e s p b -> p (e s) b").bitcast(I32))
-        load_scales(nc.sync, wbs, wb_scales.rearrange("e s r n -> r (e s) n"))
-        nc.sync.dma_start(out=w2[:].bitcast(I32), in_=w2_words[0].bitcast(I32))
-        load_scales(nc.sync, w2s, w2_scales[0])
+        load_scales((nc.sync,) * 4, wbs, wb_scales.rearrange("e s r n -> r (e s) n"))
+        load_scales((nc.sync,) * 4, w2s, w2_scales[0])
 
         pools = []
-        for name, lst, cut in (("a", list_a, 256), ("b", list_b, 384)):
+        for name, lst, cuts in (("a", list_a, (0, 256, T)), ("b", list_b, (0, T))):
             gw = keep.tile([P, T], U32, name="gw_" + name, align_bytes=64)
             gs = keep.tile([P, T], U8, name="gs_" + name, align_bytes=64)
-            for lo, hi in ((0, 384), (384, T)):
-                nc.vector.tensor_copy(gs[:, lo:hi], xs[:].indirect(offsets(lst, lo, hi)))
-            for lo, hi in ((0, cut), (cut, T)):
+            nc.vector.tensor_copy(gs[:], xs[:].indirect(lst[:]))
+            for lo, hi in zip(cuts, cuts[1:]):
                 nc.vector.tensor_copy(gw[:, lo:hi], xw[:].bitcast(U32).indirect(offsets(lst, lo, hi)))
             pools.append((gw, gs))
 
@@ -109,7 +109,7 @@ def tile_moe_pool_sigmoid_kernel(
 
         gate = [keep.tile([P, T], F32, name="gate%d" % t) for t in range(PACK)]
         lin = [keep.tile([P, WINDOW], F32, name="lin%d" % t) for t in range(PACK)]
-        for lo, hi in ((0, 256), (256, T)):
+        for lo, hi in ((0, 128), (128, 384), (384, T)):
             for t in range(PACK):
                 nc.vector.tensor_copy(gate[t][:].indirect(offsets(list_a, lo, hi)), slot_vals[0][:, t, lo:hi])
         hb = keep.tile([P, PACK, T], BF16, name="hb", align_bytes=64)
@@ -122,54 +122,69 @@ def tile_moe_pool_sigmoid_kernel(
             if t == 1:
                 nc.scalar.copy(grouped[:, :, 0:2], hb[:, 0:2, :].rearrange("p t k -> p k t"))
 
-        chunks = [slice(0, 256), slice(256, 512), slice(512, 640), slice(640, T)]
+        warm = psum.tile([P, H], F32, name="warm")
+        plane2 = hb[:, 2, :].bitcast(F32)
+        for j in range(WARM_TRANSPOSES):
+            nc.tensor.transpose(warm[:, (j % 4) * P : (j % 4 + 1) * P], plane2[:, 0:P], ident[:])
+        for j in range(3):
+            nc.tensor.matmul_mx(
+                out=warm[:], lhsT=pools[1][0][:, 0:P].bitcast(FP8X4), lhsT_scale=pools[1][1][:, 0:P],
+                rhs=wb[:, 0, :].bitcast(FP4X4), rhs_scale=wbs[:, 0, :], start=True, stop=True,
+            )
+
+        chunks = [slice(0, 128), slice(128, 384), slice(384, 512), slice(512, T)]
         out_rows = out.rearrange("(u p) t -> p u t", p=P)
 
-        def product(cols):
+        def product(c):
+            cols = chunks[c]
             nc.vector.tensor_tensor(hb[:, last, cols], gate[last][:, cols], lin[last][:, cols], MULT)
 
         def pair(c):
             dst, src = grouped[:, chunks[c], 2:4], hb[:, 2:4, chunks[c]].rearrange("p t k -> p k t")
-            if c % 2:
+            if c in (1, 2):
                 nc.scalar.copy(dst, src)
             else:
                 nc.vector.tensor_copy(dst, src)
 
-        def finish(c):
+        def quantise(c):
             cols = chunks[c]
             width = cols.stop - cols.start
             hq = keep.tile([P, width], U32, name="hq%d" % c, align_bytes=64)
             hs = keep.tile([P, width], U8, name="hs%d" % c, align_bytes=64)
             nc.vector.quantize_mx(out=hq[:].bitcast(FP8X4), scales=hs[:], in_=grouped[:, cols, :].rearrange("p k t -> p (k t)"))
-            res = psum.tile([P, 2, width], F32, name="res%d" % c)  if c < 2 else psum.tile([P, 2, width], F32, name="res%d" % c, tag="acc", bufs=3)
-            for u in range(2):
+            return hq, hs
+
+        def project(c, codes, halves, tag, engine):
+            hq, hs = codes
+            cols = chunks[c]
+            shape = [P, len(halves), cols.stop - cols.start]
+            res = psum.tile(shape, F32, name="res", tag=tag, bufs=3)
+            for j, u in enumerate(halves):
                 nc.tensor.matmul_mx(
-                    out=res[:, u, :], lhsT=w2[:, 2 * P * u : 2 * P * (u + 1)].bitcast(FP4X4), lhsT_scale=w2s[:, P * u : P * (u + 1)],
+                    out=res[:, j, :], lhsT=w2[:, 2 * P * u : 2 * P * (u + 1)].bitcast(FP4X4), lhsT_scale=w2s[:, P * u : P * (u + 1)],
                     rhs=hq[:].bitcast(FP8X4), rhs_scale=hs[:], start=True, stop=True,
                 )
-            return res
-
-        def store(c, res):
-            cols = chunks[c]
-            done = keep.tile([P, 2, cols.stop - cols.start], F32, name="done%d" % c)
-            if c < 2:
+            done = keep.tile(shape, F32, name="done%d_%d" % (c, halves[0]))
+            if engine == "scalar":
                 nc.scalar.copy(done[:], res[:])
             else:
                 nc.vector.tensor_copy(done[:], res[:])
-            nc.sync.dma_start(out=out_rows[:, :, cols], in_=done[:])
+            nc.sync.dma_start(out=out_rows[:, halves[0] : halves[-1] + 1, cols], in_=done[:])
 
-        product(chunks[0])
-        product(chunks[1])
+        product(0)
+        product(1)
         pair(0)
         pair(1)
-        product(slice(512, T))
-        res0 = finish(0)
+        product(2)
         pair(2)
+        project(0, quantise(0), (0, 1), "acc", "scalar")
+        product(3)
+        codes1 = quantise(1)
+        project(1, codes1, (0,), "acc", "scalar")
+        project(1, codes1, (1,), "turned", "scalar")
         pair(3)
-        store(0, res0)
-        res1 = finish(1)
-        store(1, res1)
-        res2 = finish(2)
-        res3 = finish(3)
-        store(2, res2)
-        store(3, res3)
+        codes2 = quantise(2)
+        codes3 = quantise(3)
+        project(2, codes2, (0, 1), "acc", "vector")
+        project(3, codes3, (0,), "turned", "vector")
+        project(3, codes3, (1,), "turned", "scalar")

from contextlib import ExitStack

import concourse.mybir as mybir
from concourse.masks import make_identity

K, T, E1, C1, E2, C2, H, N = 512, 768, 6, 128, 3, 256, 512, 256
FLOPS = 2 * T * (2 * K * H + H * N)

F32 = mybir.dt.float32
BF16 = mybir.dt.bfloat16
I32 = mybir.dt.int32
U32 = mybir.dt.uint32
U16 = mybir.dt.uint16
U8 = mybir.dt.uint8
FP8X4 = mybir.dt.float8_e4m3fn_x4
FP4X4 = mybir.dt.float4_e2m1fn_x4
SIGMOID = mybir.ActivationFunctionType.Sigmoid
MULT = mybir.AluOpType.mult

P = 128
PACK = 4
LIST_ROWS = 16
SLOT_TILES = T // P
WINDOW = 1024
WARM_TRANSPOSES = 14


def load_scales(queues, plane, rows):
    for q, queue in enumerate(queues):
        queue.dma_start(out=plane[32 * q : 32 * q + 4].bitcast(I32), in_=rows[4 * q : 4 * q + 4].bitcast(I32))


def offsets(lst, lo, hi):
    return lst[:, lo // LIST_ROWS : hi // LIST_ROWS]


def tile_moe_pool_sigmoid_kernel(
    tc, x_words, x_scales, wa_words, wa_scales, wb_words, wb_scales, w2_words, w2_scales, offs, offs2, out
):
    nc = tc.nc
    with ExitStack() as ctx:
        keep = ctx.enter_context(tc.tile_pool(name="keep", bufs=1))
        stage = ctx.enter_context(tc.tile_pool(name="stage", bufs=3))
        psum = ctx.enter_context(tc.psum_pool(name="psum", bufs=1))

        list_a = keep.tile([P, T // LIST_ROWS], U16, name="list_a")
        list_b = keep.tile([P, T // LIST_ROWS], U16, name="list_b")
        xw = keep.tile([P, WINDOW], I32, name="xw", align_bytes=64)
        xs = keep.tile([P, WINDOW], U8, name="xs", align_bytes=64)
        wa = keep.tile([P, E1, 2 * H], U8, name="wa", align_bytes=64)
        wb = keep.tile([P, E2, 2 * H], U8, name="wb", align_bytes=64)
        w2 = keep.tile([P, 2 * N], U8, name="w2", align_bytes=64)
        was = keep.tile([P, E1, H], U8, name="was", align_bytes=64)
        wbs = keep.tile([P, E2, H], U8, name="wbs", align_bytes=64)
        w2s = keep.tile([P, N], U8, name="w2s", align_bytes=64)
        ident = keep.tile([P, P], F32, name="ident")

        wa_rows = wa_words.rearrange("e s p b -> p (e s) b")
        nc.gpsimd.memset(xs[:].bitcast(I32), 0)
        nc.vector.memset(was[:].bitcast(I32), 0)
        make_identity(nc, ident[:])
        nc.gpsimd.dma_start(out=wa[:, 2:E1, :].bitcast(I32), in_=wa_rows[:, 2:E1, :].bitcast(I32))
        nc.gpsimd.memset(wbs[:].bitcast(I32), 0)
        nc.gpsimd.dma_start(out=wb[:].bitcast(I32), in_=wb_words.rearrange("e s p b -> p (e s) b").bitcast(I32))
        nc.gpsimd.memset(w2s[:].bitcast(I32), 0)
        nc.gpsimd.dma_start(out=w2[:].bitcast(I32), in_=w2_words[0].bitcast(I32))

        nc.sync.dma_start(list_a[:], offs)
        load_scales((nc.scalar, nc.scalar, nc.sync, nc.sync), xs[:, 0:T], x_scales[0])
        nc.sync.dma_start(out=xw[:, 0:T], in_=x_words.rearrange("s p t d -> p (s t d)").bitcast(I32))
        nc.sync.dma_start(out=wa[:, 0:2, :].bitcast(I32), in_=wa_rows[:, 0:2, :].bitcast(I32))
        load_scales((nc.sync,) * 4, was, wa_scales.rearrange("e s r n -> r (e s) n"))
        nc.sync.dma_start(list_b[:], offs2)
        load_scales((nc.sync,) * 4, wbs, wb_scales.rearrange("e s r n -> r (e s) n"))
        load_scales((nc.sync,) * 4, w2s, w2_scales[0])

        pools = []
        for name, lst, cuts in (("a", list_a, (0, 256, T)), ("b", list_b, (0, T))):
            gw = keep.tile([P, T], U32, name="gw_" + name, align_bytes=64)
            gs = keep.tile([P, T], U8, name="gs_" + name, align_bytes=64)
            nc.vector.tensor_copy(gs[:], xs[:].indirect(lst[:]))
            for lo, hi in zip(cuts, cuts[1:]):
                nc.vector.tensor_copy(gw[:, lo:hi], xw[:].bitcast(U32).indirect(offsets(lst, lo, hi)))
            pools.append((gw, gs))

        slot_vals = []
        for pool, (gw, gs) in enumerate(pools):
            words, scales, per = ((wa, was, C1), (wb, wbs, C2))[pool]
            vals = keep.tile([P, PACK, T], F32, name="vals%d" % pool)
            for s in range(SLOT_TILES):
                cols = slice(s * P, (s + 1) * P)
                e = s * P // per
                acc = psum.tile([P, H], F32, name="acc", tag="acc", bufs=3)
                nc.tensor.matmul_mx(
                    out=acc[:], lhsT=gw[:, cols].bitcast(FP8X4), lhsT_scale=gs[:, cols],
                    rhs=words[:, e, :].bitcast(FP4X4), rhs_scale=scales[:, e, :], start=True, stop=True,
                )
                rows = stage.tile([P, PACK, P], F32, name="rows")
                src = acc[:].rearrange("p (m t) -> p t m", t=PACK)
                if pool == 0:
                    nc.scalar.activation(rows[:], src, SIGMOID)
                else:
                    nc.scalar.copy(rows[:], src)
                turned = psum.tile([P, PACK, P], F32, name="turned", tag="turned", bufs=3)
                for t in range(PACK):
                    nc.tensor.transpose(turned[:, t, :], rows[:, t, :], ident[:])
                nc.scalar.copy(vals[:, :, cols], turned[:])
            slot_vals.append(vals)

        gate = [keep.tile([P, T], F32, name="gate%d" % t) for t in range(PACK)]
        lin = [keep.tile([P, WINDOW], F32, name="lin%d" % t) for t in range(PACK)]
        for lo, hi in ((0, 128), (128, 384), (384, T)):
            for t in range(PACK):
                nc.vector.tensor_copy(gate[t][:].indirect(offsets(list_a, lo, hi)), slot_vals[0][:, t, lo:hi])
        hb = keep.tile([P, PACK, T], BF16, name="hb", align_bytes=64)
        grouped = keep.tile([P, T, PACK], BF16, name="grouped", align_bytes=64)
        last = PACK - 1
        for t in range(PACK):
            nc.vector.tensor_copy(lin[t][:].indirect(list_b[:]), slot_vals[1][:, t, :])
            if t < last:
                nc.gpsimd.tensor_tensor(hb[:, t, :], gate[t][:], lin[t][:, 0:T], MULT)
            if t == 1:
                nc.scalar.copy(grouped[:, :, 0:2], hb[:, 0:2, :].rearrange("p t k -> p k t"))

        warm = psum.tile([P, H], F32, name="warm")
        plane2 = hb[:, 2, :].bitcast(F32)
        for j in range(WARM_TRANSPOSES):
            nc.tensor.transpose(warm[:, (j % 4) * P : (j % 4 + 1) * P], plane2[:, 0:P], ident[:])
        for j in range(3):
            nc.tensor.matmul_mx(
                out=warm[:], lhsT=pools[1][0][:, 0:P].bitcast(FP8X4), lhsT_scale=pools[1][1][:, 0:P],
                rhs=wb[:, 0, :].bitcast(FP4X4), rhs_scale=wbs[:, 0, :], start=True, stop=True,
            )

        chunks = [slice(0, 128), slice(128, 384), slice(384, 512), slice(512, T)]
        out_rows = out.rearrange("(u p) t -> p u t", p=P)

        def product(c):
            cols = chunks[c]
            nc.vector.tensor_tensor(hb[:, last, cols], gate[last][:, cols], lin[last][:, cols], MULT)

        def pair(c):
            dst, src = grouped[:, chunks[c], 2:4], hb[:, 2:4, chunks[c]].rearrange("p t k -> p k t")
            if c in (1, 2):
                nc.scalar.copy(dst, src)
            else:
                nc.vector.tensor_copy(dst, src)

        def quantise(c):
            cols = chunks[c]
            width = cols.stop - cols.start
            hq = keep.tile([P, width], U32, name="hq%d" % c, align_bytes=64)
            hs = keep.tile([P, width], U8, name="hs%d" % c, align_bytes=64)
            nc.vector.quantize_mx(out=hq[:].bitcast(FP8X4), scales=hs[:], in_=grouped[:, cols, :].rearrange("p k t -> p (k t)"))
            return hq, hs

        def project(c, codes, halves, tag, engine):
            hq, hs = codes
            cols = chunks[c]
            shape = [P, len(halves), cols.stop - cols.start]
            res = psum.tile(shape, F32, name="res", tag=tag, bufs=3)
            for j, u in enumerate(halves):
                nc.tensor.matmul_mx(
                    out=res[:, j, :], lhsT=w2[:, 2 * P * u : 2 * P * (u + 1)].bitcast(FP4X4), lhsT_scale=w2s[:, P * u : P * (u + 1)],
                    rhs=hq[:].bitcast(FP8X4), rhs_scale=hs[:], start=True, stop=True,
                )
            done = keep.tile(shape, F32, name="done%d_%d" % (c, halves[0]))
            if engine == "scalar":
                nc.scalar.copy(done[:], res[:])
            else:
                nc.vector.tensor_copy(done[:], res[:])
            nc.sync.dma_start(out=out_rows[:, halves[0] : halves[-1] + 1, cols], in_=done[:])

        product(0)
        product(1)
        pair(0)
        pair(1)
        product(2)
        pair(2)
        project(0, quantise(0), (0, 1), "acc", "scalar")
        product(3)
        codes1 = quantise(1)
        project(1, codes1, (0,), "acc", "scalar")
        project(1, codes1, (1,), "turned", "scalar")
        pair(3)
        codes2 = quantise(2)
        codes3 = quantise(3)
        project(2, codes2, (0, 1), "acc", "vector")
        project(3, codes3, (0,), "turned", "vector")
        project(3, codes3, (1,), "turned", "scalar")
